import numpy as np
import ml_dtypes


def mxq(x, axis, fmt="e4m3"):
    dtype, down = {"e4m3": (ml_dtypes.float8_e4m3fn, 7), "e5m2": (ml_dtypes.float8_e5m2, 14)}[fmt]
    v = np.moveaxis(np.asarray(x, np.float32).astype(ml_dtypes.bfloat16).astype(np.float64), axis, -1)
    blocks = v.reshape(v.shape[:-1] + (-1, 32))
    amax = np.abs(blocks).max(-1, keepdims=True)
    byte = np.maximum(np.where(amax > 0, np.frexp(amax)[1] - 1 + 127, 0) - down, 1)
    scale = np.exp2(byte - 127.0)
    codes = (blocks / scale).astype(np.float32).astype(dtype).astype(np.float64)
    return np.moveaxis((codes * scale).reshape(v.shape), -1, axis)


WIDE = False


def mx_kscale(k):
    if not WIDE:
        return np.ones(k)
    levels = np.array([10, -10, 5, -5, 0])
    if k % 512:
        return np.exp2(np.random.permutation(np.resize(levels, k // 32))).repeat(32)
    a = np.empty((k // 512, 16))
    for p in range(k // 512):
        a[p, :8] = np.random.permutation(np.resize(levels, 8))
        for g in range(8):
            far = levels[np.abs(levels - a[p, g]) >= 10]
            a[p, g + 8] = far[np.random.randint(len(far))]
    return np.exp2(a.ravel()).repeat(32)


def f64(x):
    return np.asarray(x).astype(np.float64)


def striped(idx):
    return np.tile(idx.reshape(-1, 16).T, (8, 1)).astype(np.uint16)


def unstriped(offs):
    return offs[:16].T.reshape(-1).astype(np.int64)


def relu2(v):
    return np.maximum(v, 0.0) ** 2


K, T, S, N = 2048, 1024, 512, 128


def setup_inputs():
    n = np.random.standard_normal
    s = mx_kscale(K)[:, None]
    return {
        "xT": (n((K, S)) * s).astype(np.float32),
        "w": (n((K, N)) / np.sqrt(K) / s).astype(np.float32),
        "b": (0.3 * n((N, 1))).astype(np.float32),
        "gate": np.tile(np.random.uniform(0.2, 1.0, S), (N, 1)).astype(np.float32),
        "offs": striped(np.random.permutation(T)[:S]),
    }


def reference(xT, w, b, gate, offs):
    idx = unstriped(offs)
    xq = mxq(f64(xT), 0, "e4m3")
    y = mxq(f64(w), 0, "e4m3").T @ xq
    y = relu2(y + f64(b))
    out = np.zeros((N, T))
    out[:, idx] = f64(gate) * y
    return out

@@ -1,0 +1,132 @@
+from contextlib import ExitStack
+
+import concourse.mybir as mybir
+
+K, T, S, N = 2048, 1024, 512, 128
+P = 128
+PACK = 4
+K_PASS = P * PACK
+PASSES = K // K_PASS
+FLOPS = 2 * K * S * N
+
+F32 = mybir.dt.float32
+BF16 = mybir.dt.bfloat16
+U32 = mybir.dt.uint32
+U16 = mybir.dt.uint16
+U8 = mybir.dt.uint8
+FP8X4 = mybir.dt.float8_e4m3fn_x4
+MULT = mybir.AluOpType.mult
+RELU = mybir.ActivationFunctionType.Relu
+SQUARE = mybir.ActivationFunctionType.Square
+
+HEAD_LOADS = ((0, 0, 512, 224, 512), (1, 0, 512, 224, 512))
+TAIL_LOADS = ((2, 0, 256, 128, 256), (3, 0, 256, 96, 256), (2, 256, 512, 160, 256), (3, 256, 512, 48, 128))
+GROUPS = ((0, 256), (256, 384), (384, 512))
+
+
+def tile_picked_place_lin_relu2_sub_l_kernel(tc, xT, w, b, gate, offs, out):
+    nc = tc.nc
+    with ExitStack() as ctx:
+        keep = ctx.enter_context(tc.tile_pool(name="keep", bufs=1))
+        psum = ctx.enter_context(tc.psum_pool(name="psum", bufs=1))
+
+        offsets = keep.tile([P, S // 16], U16, name="offsets")
+        bias = keep.tile([P, 1], F32, name="bias")
+        gates = keep.tile([P, S], F32, name="gates")
+        warm = keep.tile([P, 8], F32, name="warm")
+        window = keep.tile([P, T], F32, name="window")
+        w_raw = keep.tile([P, PASSES, PACK, N], F32, name="w_raw")
+        w_grouped = keep.tile([P, PASSES, N, PACK], BF16, name="w_grouped", align_bytes=64)
+        w_codes = keep.tile([P, PASSES * N], U32, name="w_codes", align_bytes=64)
+        w_scales = keep.tile([P, PASSES * N], U8, name="w_scales", align_bytes=64)
+        x_codes = [keep.tile([P, S], U32, name=f"x_codes{c}", align_bytes=64) for c in range(PASSES)]
+        x_scales = [keep.tile([P, S], U8, name=f"x_scales{c}", align_bytes=64) for c in range(PASSES)]
+        accs = [psum.tile([P, hi - lo], F32, name=f"acc{lo}") for lo, hi in GROUPS]
+
+        nc.sync.dma_start(out=w_raw[:], in_=w.rearrange("(c p j) n -> p c j n", p=P, j=PACK))
+        raws = {}
+        for n, (c, lo, hi, share, quant) in enumerate(HEAD_LOADS + TAIL_LOADS):
+            raw = keep.tile([P, PACK, hi - lo], F32, name=f"raw{c}_{lo}")
+            src = xT[c * K_PASS : (c + 1) * K_PASS, lo:hi]
+            nc.sync.dma_start(out=raw[:], in_=src.rearrange("(p j) s -> p j s", j=PACK))
+            raws[(c, lo)] = raw
+            if n == 0:
+                nc.sync.dma_start(offsets[:], offs)
+                nc.sync.dma_start(out=bias[:], in_=b)
+                nc.sync.dma_start(out=gates[:], in_=gate)
+
+        nc.vector.memset(warm[:], 0.0)
+        nc.scalar.activation(out=warm[:, 0:1], in_=warm[:, 1:2], func=RELU)
+        nc.vector.memset(window[:], 0.0)
+
+        half = PASSES // 2
+        nc.scalar.copy(out=w_grouped[:, :half], in_=w_raw[:, :half].rearrange("p c j n -> p c n j"))
+        nc.vector.tensor_copy(out=w_grouped[:, half:], in_=w_raw[:, half:].rearrange("p c j n -> p c n j"))
+        nc.vector.quantize_mx(
+            out=w_codes[:].bitcast(FP8X4),
+            scales=w_scales[:],
+            in_=w_grouped[:].rearrange("p c n j -> p (c n j)"),
+        )
+
+        def quantize(c, lo, hi, share, quant):
+            raw = raws[(c, lo)]
+            grouped = keep.tile([P, hi - lo, PACK], BF16, name=f"grouped{c}_{lo}", align_bytes=64)
+            for q in range(0, hi - lo, quant):
+                mid = q + share
+                nc.scalar.copy(out=grouped[:, q:mid], in_=raw[:, :, q:mid].rearrange("p j s -> p s j"))
+                nc.vector.tensor_copy(
+                    out=grouped[:, mid : q + quant], in_=raw[:, :, mid : q + quant].rearrange("p j s -> p s j")
+                )
+            for q in range(0, hi - lo, quant):
+                cols = slice(lo + q, lo + q + quant)
+                nc.vector.quantize_mx(
+                    out=x_codes[c][:, cols].bitcast(FP8X4),
+                    scales=x_scales[c][:, cols],
+                    in_=grouped[:, q : q + quant].rearrange("p s j -> p (s j)"),
+                )
+
+        def multiply(c, g):
+            lo, hi = GROUPS[g]
+            w_cols = slice(c * N, (c + 1) * N)
+            nc.tensor.matmul_mx(
+                out=accs[g][:],
+                lhsT=w_codes[:, w_cols].bitcast(FP8X4),
+                lhsT_scale=w_scales[:, w_cols],
+                rhs=x_codes[c][:, lo:hi].bitcast(FP8X4),
+                rhs_scale=x_scales[c][:, lo:hi],
+                start=(c == 0),
+                stop=(c == PASSES - 1),
+            )
+
+        def activate(g):
+            lo, hi = GROUPS[g]
+            relu = keep.tile([P, hi - lo], F32, name=f"relu{lo}")
+            relu2 = keep.tile([P, hi - lo], F32, name=f"relu2{lo}")
+            nc.scalar.activation(out=relu[:], in_=accs[g][:], func=RELU, bias=bias[:])
+            nc.scalar.activation(out=relu2[:], in_=relu[:], func=SQUARE)
+            return relu2
+
+        def scatter(g, relu2):
+            lo, hi = GROUPS[g]
+            nc.vector.tensor_tensor(
+                window[:].indirect(offsets[:, lo // 16 : hi // 16]), relu2[:], gates[:, lo:hi], MULT
+            )
+
+        for load in HEAD_LOADS:
+            quantize(*load)
+            for g in range(len(GROUPS)):
+                multiply(load[0], g)
+        for load in TAIL_LOADS:
+            c, lo, hi = load[:3]
+            quantize(*load)
+            done = []
+            for g, (g_lo, g_hi) in enumerate(GROUPS):
+                if lo <= g_lo and g_hi <= hi:
+                    multiply(c, g)
+                    done.append(g)
+            if c == PASSES - 1:
+                results = [activate(g) for g in done]
+                for g, relu2 in zip(done, results):
+                    scatter(g, relu2)
+
+        nc.sync.dma_start(out=out, in_=window[:])

@@ -19,9 +19,23 @@ MULT = mybir.AluOpType.mult
 RELU = mybir.ActivationFunctionType.Relu
 SQUARE = mybir.ActivationFunctionType.Square
 
-HEAD_LOADS = ((0, 0, 512, 224, 512), (1, 0, 512, 224, 512))
-TAIL_LOADS = ((2, 0, 256, 128, 256), (3, 0, 256, 96, 256), (2, 256, 512, 160, 256), (3, 256, 512, 48, 128))
-GROUPS = ((0, 256), (256, 384), (384, 512))
+STEPS = (
+    ("w", 0, 2, 0, 128, 0),
+    ("small", 0, 0, 0, 0, 0),
+    ("x", 0, 2, 0, 128, 128),
+    ("w", 2, 4, 0, 128, 0),
+    ("x", 2, 4, 0, 128, 128),
+    ("gate", 0, 0, 0, 512, 0),
+    ("x", 0, 2, 128, 256, 0),
+    ("x", 2, 4, 128, 256, 128),
+    ("x", 0, 2, 256, 384, 0),
+    ("x", 2, 4, 256, 384, 128),
+    ("x", 0, 2, 384, 512, 0),
+    ("x", 2, 3, 384, 512, 128),
+    ("x", 3, 4, 384, 512, 48),
+)
+GROUPS = ((0, 128), (128, 256), (256, 384), (384, 512))
+SCATTER = 128
 
 
 def tile_picked_place_lin_relu2_sub_l_kernel(tc, xT, w, b, gate, offs, out):
@@ -35,98 +49,104 @@ def tile_picked_place_lin_relu2_sub_l_kernel(tc, xT, w, b, gate, offs, out):
         gates = keep.tile([P, S], F32, name="gates")
         warm = keep.tile([P, 8], F32, name="warm")
         window = keep.tile([P, T], F32, name="window")
-        w_raw = keep.tile([P, PASSES, PACK, N], F32, name="w_raw")
-        w_grouped = keep.tile([P, PASSES, N, PACK], BF16, name="w_grouped", align_bytes=64)
-        w_codes = keep.tile([P, PASSES * N], U32, name="w_codes", align_bytes=64)
-        w_scales = keep.tile([P, PASSES * N], U8, name="w_scales", align_bytes=64)
-        x_codes = [keep.tile([P, S], U32, name=f"x_codes{c}", align_bytes=64) for c in range(PASSES)]
-        x_scales = [keep.tile([P, S], U8, name=f"x_scales{c}", align_bytes=64) for c in range(PASSES)]
         accs = [psum.tile([P, hi - lo], F32, name=f"acc{lo}") for lo, hi in GROUPS]
 
-        nc.sync.dma_start(out=w_raw[:], in_=w.rearrange("(c p j) n -> p c j n", p=P, j=PACK))
+        w_view = w.rearrange("(c p j) n -> c p j n", p=P, j=PACK)
+        x_view = xT.rearrange("(c p j) s -> c p j s", p=P, j=PACK)
         raws = {}
-        for n, (c, lo, hi, share, quant) in enumerate(HEAD_LOADS + TAIL_LOADS):
-            raw = keep.tile([P, PACK, hi - lo], F32, name=f"raw{c}_{lo}")
-            src = xT[c * K_PASS : (c + 1) * K_PASS, lo:hi]
-            nc.sync.dma_start(out=raw[:], in_=src.rearrange("(p j) s -> p j s", j=PACK))
-            raws[(c, lo)] = raw
-            if n == 0:
+        for n, (what, c_lo, c_hi, lo, hi, share) in enumerate(STEPS):
+            if what == "small":
                 nc.sync.dma_start(offsets[:], offs)
                 nc.sync.dma_start(out=bias[:], in_=b)
-                nc.sync.dma_start(out=gates[:], in_=gate)
+            elif what == "gate":
+                nc.sync.dma_start(out=gates[:, lo:hi], in_=gate[:, lo:hi])
+            else:
+                view = w_view if what == "w" else x_view
+                raw = keep.tile([P, c_hi - c_lo, PACK, hi - lo], F32, name=f"raw_{what}{c_lo}_{lo}")
+                for c in range(c_lo, c_hi):
+                    nc.sync.dma_start(out=raw[:, c - c_lo], in_=view[c, :, :, lo:hi])
+                raws[n] = raw
 
         nc.vector.memset(warm[:], 0.0)
         nc.scalar.activation(out=warm[:, 0:1], in_=warm[:, 1:2], func=RELU)
-        nc.vector.memset(window[:], 0.0)
+        nc.gpsimd.memset(window[:], 0.0)
 
-        half = PASSES // 2
-        nc.scalar.copy(out=w_grouped[:, :half], in_=w_raw[:, :half].rearrange("p c j n -> p c n j"))
-        nc.vector.tensor_copy(out=w_grouped[:, half:], in_=w_raw[:, half:].rearrange("p c j n -> p c n j"))
-        nc.vector.quantize_mx(
-            out=w_codes[:].bitcast(FP8X4),
-            scales=w_scales[:],
-            in_=w_grouped[:].rearrange("p c n j -> p (c n j)"),
-        )
+        w_parts = {}
+        x_parts = {}
 
-        def quantize(c, lo, hi, share, quant):
-            raw = raws[(c, lo)]
-            grouped = keep.tile([P, hi - lo, PACK], BF16, name=f"grouped{c}_{lo}", align_bytes=64)
-            for q in range(0, hi - lo, quant):
-                mid = q + share
-                nc.scalar.copy(out=grouped[:, q:mid], in_=raw[:, :, q:mid].rearrange("p j s -> p s j"))
+        def quantize(n):
+            what, c_lo, c_hi, lo, hi, share = STEPS[n]
+            raw = raws[n]
+            width = hi - lo
+            passes = c_hi - c_lo
+            grouped = keep.tile([P, passes, width, PACK], BF16, name=f"grouped_{what}{c_lo}_{lo}", align_bytes=64)
+            codes = keep.tile([P, passes * width], U32, name=f"codes_{what}{c_lo}_{lo}", align_bytes=64)
+            scales = keep.tile([P, passes * width], U8, name=f"scales_{what}{c_lo}_{lo}", align_bytes=64)
+            if share > 0:
+                nc.scalar.copy(out=grouped[:, :, :share], in_=raw[:, :, :, :share].rearrange("p c j s -> p c s j"))
+            if share < width:
                 nc.vector.tensor_copy(
-                    out=grouped[:, mid : q + quant], in_=raw[:, :, mid : q + quant].rearrange("p j s -> p s j")
+                    out=grouped[:, :, share:], in_=raw[:, :, :, share:].rearrange("p c j s -> p c s j")
                 )
-            for q in range(0, hi - lo, quant):
-                cols = slice(lo + q, lo + q + quant)
-                nc.vector.quantize_mx(
-                    out=x_codes[c][:, cols].bitcast(FP8X4),
-                    scales=x_scales[c][:, cols],
-                    in_=grouped[:, q : q + quant].rearrange("p s j -> p (s j)"),
-                )
+            nc.vector.quantize_mx(
+                out=codes[:].bitcast(FP8X4), scales=scales[:], in_=grouped[:].rearrange("p c s j -> p (c s j)")
+            )
+            for c in range(c_lo, c_hi):
+                part = (codes, scales, (c - c_lo) * width)
+                if what == "w":
+                    w_parts[c] = part
+                else:
+                    x_parts[(c, lo)] = part
 
-        def multiply(c, g):
+        def multiply(c, x_lo, g):
             lo, hi = GROUPS[g]
-            w_cols = slice(c * N, (c + 1) * N)
+            w_codes, w_scales, w_at = w_parts[c]
+            x_codes, x_scales, x_at = x_parts[(c, x_lo)]
+            w_cols = slice(w_at, w_at + N)
+            x_cols = slice(x_at + lo - x_lo, x_at + hi - x_lo)
             nc.tensor.matmul_mx(
                 out=accs[g][:],
                 lhsT=w_codes[:, w_cols].bitcast(FP8X4),
                 lhsT_scale=w_scales[:, w_cols],
-                rhs=x_codes[c][:, lo:hi].bitcast(FP8X4),
-                rhs_scale=x_scales[c][:, lo:hi],
+                rhs=x_codes[:, x_cols].bitcast(FP8X4),
+                rhs_scale=x_scales[:, x_cols],
                 start=(c == 0),
                 stop=(c == PASSES - 1),
             )
 
+        pending = []
+
         def activate(g):
             lo, hi = GROUPS[g]
-            relu = keep.tile([P, hi - lo], F32, name=f"relu{lo}")
-            relu2 = keep.tile([P, hi - lo], F32, name=f"relu2{lo}")
+            relu = keep.tile([P, hi - lo], F32, name=f"relu_{lo}")
+            relu2 = keep.tile([P, hi - lo], F32, name=f"relu2_{lo}")
             nc.scalar.activation(out=relu[:], in_=accs[g][:], func=RELU, bias=bias[:])
             nc.scalar.activation(out=relu2[:], in_=relu[:], func=SQUARE)
-            return relu2
+            for q in range(lo, hi, SCATTER):
+                pending.append((relu2[:, q - lo : q - lo + SCATTER], q, q + SCATTER))
 
-        def scatter(g, relu2):
-            lo, hi = GROUPS[g]
+        def scatter_one():
+            relu2, lo, hi = pending.pop(0)
             nc.vector.tensor_tensor(
-                window[:].indirect(offsets[:, lo // 16 : hi // 16]), relu2[:], gates[:, lo:hi], MULT
+                window[:].indirect(offsets[:, lo // 16 : hi // 16]), relu2, gates[:, lo:hi], MULT
             )
 
-        for load in HEAD_LOADS:
-            quantize(*load)
-            for g in range(len(GROUPS)):
-                multiply(load[0], g)
-        for load in TAIL_LOADS:
-            c, lo, hi = load[:3]
-            quantize(*load)
-            done = []
-            for g, (g_lo, g_hi) in enumerate(GROUPS):
-                if lo <= g_lo and g_hi <= hi:
-                    multiply(c, g)
-                    done.append(g)
-            if c == PASSES - 1:
-                results = [activate(g) for g in done]
-                for g, relu2 in zip(done, results):
-                    scatter(g, relu2)
+        waiting = []
+        for n, (what, c_lo, c_hi, lo, hi, share) in enumerate(STEPS):
+            if what in ("small", "gate"):
+                continue
+            quantize(n)
+            if pending:
+                scatter_one()
+            if what == "x":
+                waiting.extend((c, lo, g) for c in range(c_lo, c_hi) for g in range(len(GROUPS)) if lo <= GROUPS[g][0] < hi)
+            ready = [item for item in waiting if item[0] in w_parts]
+            waiting = [item for item in waiting if item[0] not in w_parts]
+            for c, x_lo, g in ready:
+                multiply(c, x_lo, g)
+                if c == PASSES - 1:
+                    activate(g)
+        while pending:
+            scatter_one()
 
         nc.sync.dma_start(out=out, in_=window[:])

@@ -20,19 +20,22 @@ RELU = mybir.ActivationFunctionType.Relu
 SQUARE = mybir.ActivationFunctionType.Square
 
 STEPS = (
-    ("w", 0, 2, 0, 128, 0),
+    ("w", 0, 2, 0, 128, 96),
     ("small", 0, 0, 0, 0, 0),
-    ("x", 0, 2, 0, 128, 128),
-    ("w", 2, 4, 0, 128, 0),
-    ("x", 2, 4, 0, 128, 128),
+    ("x", 0, 1, 0, 128, 96),
+    ("w", 2, 4, 0, 128, 32),
+    ("x", 1, 2, 0, 256, 128),
+    ("x", 2, 3, 0, 256, 112),
+    ("x", 3, 4, 0, 256, 128),
+    ("x", 0, 1, 128, 256, 64),
+    ("x", 0, 1, 256, 512, 0),
+    ("x", 1, 2, 256, 384, 128),
     ("gate", 0, 0, 0, 512, 0),
-    ("x", 0, 2, 128, 256, 0),
-    ("x", 2, 4, 128, 256, 128),
-    ("x", 0, 2, 256, 384, 0),
-    ("x", 2, 4, 256, 384, 128),
-    ("x", 0, 2, 384, 512, 0),
-    ("x", 2, 3, 384, 512, 128),
-    ("x", 3, 4, 384, 512, 48),
+    ("x", 2, 3, 256, 384, 128),
+    ("x", 3, 4, 256, 384, 128),
+    ("x", 1, 2, 384, 512, 128),
+    ("x", 2, 3, 384, 512, 56),
+    ("x", 3, 4, 384, 512, 56),
 )
 GROUPS = ((0, 128), (128, 256), (256, 384), (384, 512))
 SCATTER = 128
@@ -98,6 +101,8 @@ def tile_picked_place_lin_relu2_sub_l_kernel(tc, xT, w, b, gate, offs, out):
                 else:
                     x_parts[(c, lo)] = part
 
+        products = [0] * len(GROUPS)
+
         def multiply(c, x_lo, g):
             lo, hi = GROUPS[g]
             w_codes, w_scales, w_at = w_parts[c]
@@ -110,9 +115,10 @@ def tile_picked_place_lin_relu2_sub_l_kernel(tc, xT, w, b, gate, offs, out):
                 lhsT_scale=w_scales[:, w_cols],
                 rhs=x_codes[:, x_cols].bitcast(FP8X4),
                 rhs_scale=x_scales[:, x_cols],
-                start=(c == 0),
-                stop=(c == PASSES - 1),
+                start=(products[g] == 0),
+                stop=(products[g] == PASSES - 1),
             )
+            products[g] += 1
 
         pending = []
 
@@ -144,7 +150,7 @@ def tile_picked_place_lin_relu2_sub_l_kernel(tc, xT, w, b, gate, offs, out):
             waiting = [item for item in waiting if item[0] not in w_parts]
             for c, x_lo, g in ready:
                 multiply(c, x_lo, g)
-                if c == PASSES - 1:
+                if products[g] == PASSES:
                     activate(g)
         while pending:
             scatter_one()

@@ -85,12 +85,16 @@ def tile_picked_place_lin_relu2_sub_l_kernel(tc, xT, w, b, gate, offs, out):
             grouped = keep.tile([P, passes, width, PACK], BF16, name=f"grouped_{what}{c_lo}_{lo}", align_bytes=64)
             codes = keep.tile([P, passes * width], U32, name=f"codes_{what}{c_lo}_{lo}", align_bytes=64)
             scales = keep.tile([P, passes * width], U8, name=f"scales_{what}{c_lo}_{lo}", align_bytes=64)
-            if share > 0:
-                nc.scalar.copy(out=grouped[:, :, :share], in_=raw[:, :, :, :share].rearrange("p c j s -> p c s j"))
-            if share < width:
-                nc.vector.tensor_copy(
-                    out=grouped[:, :, share:], in_=raw[:, :, :, share:].rearrange("p c j s -> p c s j")
-                )
+            for copy, a, b in ((nc.scalar.copy, 0, share), (nc.vector.tensor_copy, share, width)):
+                if a == b:
+                    continue
+                if passes == 1:
+                    copy(
+                        out=grouped[:, 0, a:b].rearrange("p (s i) j -> p s j i", i=4),
+                        in_=raw[:, 0, :, a:b].rearrange("p j (s i) -> p s j i", i=4),
+                    )
+                else:
+                    copy(out=grouped[:, :, a:b], in_=raw[:, :, :, a:b].rearrange("p c j s -> p c s j"))
             nc.vector.quantize_mx(
                 out=codes[:].bitcast(FP8X4), scales=scales[:], in_=grouped[:].rearrange("p c s j -> p (c s j)")
             )

@@ -20,22 +20,22 @@ RELU = mybir.ActivationFunctionType.Relu
 SQUARE = mybir.ActivationFunctionType.Square
 
 STEPS = (
-    ("w", 0, 2, 0, 128, 96),
+    ("w", 0, 2, 0, 128, 48),
     ("small", 0, 0, 0, 0, 0),
-    ("x", 0, 1, 0, 128, 96),
-    ("w", 2, 4, 0, 128, 32),
-    ("x", 1, 2, 0, 256, 128),
-    ("x", 2, 3, 0, 256, 112),
-    ("x", 3, 4, 0, 256, 128),
-    ("x", 0, 1, 128, 256, 64),
-    ("x", 0, 1, 256, 512, 0),
-    ("x", 1, 2, 256, 384, 128),
+    ("w", 2, 4, 0, 128, 48),
+    ("x", 0, 1, 0, 256, 96),
+    ("x", 1, 2, 0, 256, 112),
+    ("x", 2, 3, 0, 128, 64),
+    ("x", 3, 4, 0, 128, 128),
+    ("x", 2, 3, 128, 256, 56),
+    ("x", 3, 4, 128, 256, 72),
+    ("x", 2, 3, 256, 384, 56),
     ("gate", 0, 0, 0, 512, 0),
-    ("x", 2, 3, 256, 384, 128),
-    ("x", 3, 4, 256, 384, 128),
+    ("x", 0, 2, 256, 384, 128),
+    ("x", 3, 4, 256, 512, 96),
+    ("x", 0, 1, 384, 512, 128),
     ("x", 1, 2, 384, 512, 128),
-    ("x", 2, 3, 384, 512, 56),
-    ("x", 3, 4, 384, 512, 56),
+    ("x", 2, 3, 384, 512, 0),
 )
 GROUPS = ((0, 128), (128, 256), (256, 384), (384, 512))
 SCATTER = 128

from contextlib import ExitStack

import concourse.mybir as mybir

K, T, S, N = 2048, 1024, 512, 128
P = 128
PACK = 4
K_PASS = P * PACK
PASSES = K // K_PASS
FLOPS = 2 * K * S * N

F32 = mybir.dt.float32
BF16 = mybir.dt.bfloat16
U32 = mybir.dt.uint32
U16 = mybir.dt.uint16
U8 = mybir.dt.uint8
FP8X4 = mybir.dt.float8_e4m3fn_x4
MULT = mybir.AluOpType.mult
RELU = mybir.ActivationFunctionType.Relu
SQUARE = mybir.ActivationFunctionType.Square

STEPS = (
    ("w", 0, 2, 0, 128, 48),
    ("small", 0, 0, 0, 0, 0),
    ("w", 2, 4, 0, 128, 48),
    ("x", 0, 1, 0, 256, 96),
    ("x", 1, 2, 0, 256, 112),
    ("x", 2, 3, 0, 128, 64),
    ("x", 3, 4, 0, 128, 128),
    ("x", 2, 3, 128, 256, 56),
    ("x", 3, 4, 128, 256, 72),
    ("x", 2, 3, 256, 384, 56),
    ("gate", 0, 0, 0, 512, 0),
    ("x", 0, 2, 256, 384, 128),
    ("x", 3, 4, 256, 512, 96),
    ("x", 0, 1, 384, 512, 128),
    ("x", 1, 2, 384, 512, 128),
    ("x", 2, 3, 384, 512, 0),
)
GROUPS = ((0, 128), (128, 256), (256, 384), (384, 512))
SCATTER = 128


def tile_picked_place_lin_relu2_sub_l_kernel(tc, xT, w, b, gate, offs, out):
    nc = tc.nc
    with ExitStack() as ctx:
        keep = ctx.enter_context(tc.tile_pool(name="keep", bufs=1))
        psum = ctx.enter_context(tc.psum_pool(name="psum", bufs=1))

        offsets = keep.tile([P, S // 16], U16, name="offsets")
        bias = keep.tile([P, 1], F32, name="bias")
        gates = keep.tile([P, S], F32, name="gates")
        warm = keep.tile([P, 8], F32, name="warm")
        window = keep.tile([P, T], F32, name="window")
        accs = [psum.tile([P, hi - lo], F32, name=f"acc{lo}") for lo, hi in GROUPS]

        w_view = w.rearrange("(c p j) n -> c p j n", p=P, j=PACK)
        x_view = xT.rearrange("(c p j) s -> c p j s", p=P, j=PACK)
        raws = {}
        for n, (what, c_lo, c_hi, lo, hi, share) in enumerate(STEPS):
            if what == "small":
                nc.sync.dma_start(offsets[:], offs)
                nc.sync.dma_start(out=bias[:], in_=b)
            elif what == "gate":
                nc.sync.dma_start(out=gates[:, lo:hi], in_=gate[:, lo:hi])
            else:
                view = w_view if what == "w" else x_view
                raw = keep.tile([P, c_hi - c_lo, PACK, hi - lo], F32, name=f"raw_{what}{c_lo}_{lo}")
                for c in range(c_lo, c_hi):
                    nc.sync.dma_start(out=raw[:, c - c_lo], in_=view[c, :, :, lo:hi])
                raws[n] = raw

        nc.vector.memset(warm[:], 0.0)
        nc.scalar.activation(out=warm[:, 0:1], in_=warm[:, 1:2], func=RELU)
        nc.gpsimd.memset(window[:], 0.0)

        w_parts = {}
        x_parts = {}

        def quantize(n):
            what, c_lo, c_hi, lo, hi, share = STEPS[n]
            raw = raws[n]
            width = hi - lo
            passes = c_hi - c_lo
            grouped = keep.tile([P, passes, width, PACK], BF16, name=f"grouped_{what}{c_lo}_{lo}", align_bytes=64)
            codes = keep.tile([P, passes * width], U32, name=f"codes_{what}{c_lo}_{lo}", align_bytes=64)
            scales = keep.tile([P, passes * width], U8, name=f"scales_{what}{c_lo}_{lo}", align_bytes=64)
            for copy, a, b in ((nc.scalar.copy, 0, share), (nc.vector.tensor_copy, share, width)):
                if a == b:
                    continue
                if passes == 1:
                    copy(
                        out=grouped[:, 0, a:b].rearrange("p (s i) j -> p s j i", i=4),
                        in_=raw[:, 0, :, a:b].rearrange("p j (s i) -> p s j i", i=4),
                    )
                else:
                    copy(out=grouped[:, :, a:b], in_=raw[:, :, :, a:b].rearrange("p c j s -> p c s j"))
            nc.vector.quantize_mx(
                out=codes[:].bitcast(FP8X4), scales=scales[:], in_=grouped[:].rearrange("p c s j -> p (c s j)")
            )
            for c in range(c_lo, c_hi):
                part = (codes, scales, (c - c_lo) * width)
                if what == "w":
                    w_parts[c] = part
                else:
                    x_parts[(c, lo)] = part

        products = [0] * len(GROUPS)

        def multiply(c, x_lo, g):
            lo, hi = GROUPS[g]
            w_codes, w_scales, w_at = w_parts[c]
            x_codes, x_scales, x_at = x_parts[(c, x_lo)]
            w_cols = slice(w_at, w_at + N)
            x_cols = slice(x_at + lo - x_lo, x_at + hi - x_lo)
            nc.tensor.matmul_mx(
                out=accs[g][:],
                lhsT=w_codes[:, w_cols].bitcast(FP8X4),
                lhsT_scale=w_scales[:, w_cols],
                rhs=x_codes[:, x_cols].bitcast(FP8X4),
                rhs_scale=x_scales[:, x_cols],
                start=(products[g] == 0),
                stop=(products[g] == PASSES - 1),
            )
            products[g] += 1

        pending = []

        def activate(g):
            lo, hi = GROUPS[g]
            relu = keep.tile([P, hi - lo], F32, name=f"relu_{lo}")
            relu2 = keep.tile([P, hi - lo], F32, name=f"relu2_{lo}")
            nc.scalar.activation(out=relu[:], in_=accs[g][:], func=RELU, bias=bias[:])
            nc.scalar.activation(out=relu2[:], in_=relu[:], func=SQUARE)
            for q in range(lo, hi, SCATTER):
                pending.append((relu2[:, q - lo : q - lo + SCATTER], q, q + SCATTER))

        def scatter_one():
            relu2, lo, hi = pending.pop(0)
            nc.vector.tensor_tensor(
                window[:].indirect(offsets[:, lo // 16 : hi // 16]), relu2, gates[:, lo:hi], MULT
            )

        waiting = []
        for n, (what, c_lo, c_hi, lo, hi, share) in enumerate(STEPS):
            if what in ("small", "gate"):
                continue
            quantize(n)
            if pending:
                scatter_one()
            if what == "x":
                waiting.extend((c, lo, g) for c in range(c_lo, c_hi) for g in range(len(GROUPS)) if lo <= GROUPS[g][0] < hi)
            ready = [item for item in waiting if item[0] in w_parts]
            waiting = [item for item in waiting if item[0] not in w_parts]
            for c, x_lo, g in ready:
                multiply(c, x_lo, g)
                if products[g] == PASSES:
                    activate(g)
        while pending:
            scatter_one()

        nc.sync.dma_start(out=out, in_=window[:])
